import numpy as np
import ml_dtypes


def mxq(x, axis, fmt="e4m3"):
    dtype, down = {"e4m3": (ml_dtypes.float8_e4m3fn, 7), "e5m2": (ml_dtypes.float8_e5m2, 14)}[fmt]
    v = np.moveaxis(np.asarray(x, np.float32).astype(ml_dtypes.bfloat16).astype(np.float64), axis, -1)
    blocks = v.reshape(v.shape[:-1] + (-1, 32))
    amax = np.abs(blocks).max(-1, keepdims=True)
    byte = np.maximum(np.where(amax > 0, np.frexp(amax)[1] - 1 + 127, 0) - down, 1)
    scale = np.exp2(byte - 127.0)
    codes = (blocks / scale).astype(np.float32).astype(dtype).astype(np.float64)
    return np.moveaxis((codes * scale).reshape(v.shape), -1, axis)


WIDE = False


def mx_kscale(k):
    if not WIDE:
        return np.ones(k)
    levels = np.array([10, -10, 5, -5, 0])
    if k % 512:
        return np.exp2(np.random.permutation(np.resize(levels, k // 32))).repeat(32)
    a = np.empty((k // 512, 16))
    for p in range(k // 512):
        a[p, :8] = np.random.permutation(np.resize(levels, 8))
        for g in range(8):
            far = levels[np.abs(levels - a[p, g]) >= 10]
            a[p, g + 8] = far[np.random.randint(len(far))]
    return np.exp2(a.ravel()).repeat(32)


def f64(x):
    return np.asarray(x).astype(np.float64)


def striped(idx):
    return np.tile(idx.reshape(-1, 16).T, (8, 1)).astype(np.uint16)


def unstriped(offs):
    return offs[:16].T.reshape(-1).astype(np.int64)


def striped8(idx):
    return np.concatenate([x.reshape(-1, 16).T for x in idx]).astype(np.uint16)


def runs(offs, k):
    lists = np.stack([offs[16 * r : 16 * r + 16].T.reshape(-1) for r in range(8)]).astype(np.int64)
    return lists[np.arange(k) % 512 // 64]


def pack_weight(w):
    k, n = w.shape
    w = f64(np.asarray(w, np.float32).astype(ml_dtypes.bfloat16)).reshape(k // 32, 32, n)
    amax = np.abs(w).max(1)
    byte = np.clip(np.where(amax > 0, np.frexp(amax)[1] - 1 + 127 - 7, 1), 1, 254)
    scaled = (w * np.exp2(127.0 - byte)[:, None, :]).reshape(k, n).astype(np.float32)
    words = np.ascontiguousarray(scaled.reshape(k // 512, 128, 4, n).transpose(0, 1, 3, 2)).astype(ml_dtypes.float8_e4m3fn).view(np.uint8)
    return words, np.ascontiguousarray(byte.astype(np.uint8).reshape(k // 512, 16, n))


def unpack_weight(words, scales):
    g, p, n, _ = words.shape
    vals = np.ascontiguousarray(words).view(ml_dtypes.float8_e4m3fn).astype(np.float64) * np.repeat(np.exp2(scales.astype(np.float64) - 127.0), 8, axis=1)[..., None]
    return vals.transpose(0, 1, 3, 2).reshape(g * 512, n)


def sigmoid(v):
    return 1.0 / (1.0 + np.exp(-np.maximum(v, -700.0)))

def planes(y):
    n, m = y.shape
    v = y.astype(np.float32).astype(ml_dtypes.bfloat16).astype(np.float64).reshape(n // 32, 32, m)
    top = np.abs(v).max(1)
    byte = np.clip(np.where(top > 0, np.frexp(top)[1] - 1 + 127 - 7, 1), 1, 254)
    codes = (v * np.exp2(127.0 - byte)[:, None, :]).reshape(n, m).astype(np.float32).astype(ml_dtypes.float8_e4m3fn).view(np.uint8)
    words = codes.reshape(n // 512, 128, 4, m).transpose(0, 1, 3, 2)
    return np.ascontiguousarray(words), np.ascontiguousarray(byte.astype(np.uint8).reshape(n // 512, 16, m))


K, T, S, N, G, H = 512, 2048, 512, 512, 2048, 512


def setup_inputs():
    n = np.random.standard_normal
    s = mx_kscale(K)[:, None]
    u = mx_kscale(H)
    packed_xT = pack_weight(n((K, T)) * s)
    packed_dT = pack_weight(n((K, G)) / s)
    packed_w1 = pack_weight(n((H, N)) / np.sqrt(H) / u[:, None])
    return {
        "x_words": packed_xT[0],
        "x_scales": packed_xT[1],
        "d_words": packed_dT[0],
        "d_scales": packed_dT[1],
        "gn": (np.random.uniform(0.5, 1.5, (H, 1)) * u[:, None]).astype(np.float32),
        "w1_words": packed_w1[0],
        "w1_scales": packed_w1[1],
        "offs": striped(np.random.permutation(T)[:S]),
        "kidx": striped8(np.random.randint(0, G, (8, H))),
        "n1": striped8(np.stack([np.random.permutation(S) for _ in range(8)])),
        "n2": striped8(np.stack([np.random.permutation(S) for _ in range(8)])),
    }


def reference(x_words, x_scales, d_words, d_scales, gn, w1_words, w1_scales, offs, kidx, n1, n2):
    d_kidx = unpack_weight(d_words, d_scales)[np.arange(K)[:, None], runs(kidx, K)]
    xq = unpack_weight(x_words, x_scales)[:, unstriped(offs)]
    s = 0.0625 * (d_kidx.T @ xq)
    sg = sigmoid(s[np.arange(H)[:, None], runs(n1, H)] - (s[np.arange(H)[:, None], runs(n2, H)]))
    z = f64(gn) * (s * sg)
    out_0 = unpack_weight(w1_words, w1_scales).T @ mxq(z, 0, "e4m3")
    return (out_0,) + planes(out_0)

@@ -1,0 +1,198 @@
+from contextlib import ExitStack
+
+import concourse.mybir as mybir
+
+F32 = mybir.dt.float32
+BF16 = mybir.dt.bfloat16
+I32 = mybir.dt.int32
+U32 = mybir.dt.uint32
+U16 = mybir.dt.uint16
+U8 = mybir.dt.uint8
+FP8X4 = mybir.dt.float8_e4m3fn_x4
+ACT = mybir.ActivationFunctionType
+ALU = mybir.AluOpType
+
+P = 128
+PACK = 4
+TABLE = 2048
+S = 512
+LIST_ROWS = 16
+CHUNKS = (256, 128, 128)
+FLOPS = 2 * 2 * 512 * 512 * 512
+
+
+def tile_picked_scorecmp_none_po_kernel(
+    tc, x_words, x_scales, d_words, d_scales, gn, w1_words, w1_scales, offs, kidx, n1, n2, out_0, out_1, out_2
+):
+    nc = tc.nc
+    with ExitStack() as ctx:
+        keep = ctx.enter_context(tc.tile_pool(name="keep", bufs=1))
+        psum = ctx.enter_context(tc.psum_pool(name="psum", bufs=1))
+
+        def words_of(dram):
+            return dram[0].rearrange("p c r -> p (c r)").bitcast(I32)
+
+        kidx_sb = keep.tile([P, S // LIST_ROWS], U16, name="kidx_sb")
+        offs_sb = keep.tile([P, S // LIST_ROWS], U16, name="offs_sb")
+        n1_sb = keep.tile([P, S // LIST_ROWS], U16, name="n1_sb")
+        n2_sb = keep.tile([P, S // LIST_ROWS], U16, name="n2_sb")
+        d_tab = keep.tile([P, TABLE], I32, name="d_tab", align_bytes=64)
+        x_tab = keep.tile([P, TABLE], I32, name="x_tab", align_bytes=64)
+        dsc_tab = keep.tile([P, TABLE], U8, name="dsc_tab", tag="dsc_then_w", align_bytes=64)
+        xsc_tab = keep.tile([P, TABLE], U8, name="xsc_tab", align_bytes=64)
+        warm_in = keep.tile([P, 1], F32, name="warm_in")
+        warm_out = keep.tile([P, 1], F32, name="warm_out")
+
+        nc.gpsimd.memset(dsc_tab[:].bitcast(I32), 0)
+        nc.vector.memset(xsc_tab[:].bitcast(I32), 0)
+        nc.vector.memset(warm_in[:], 0.0)
+        nc.scalar.activation(warm_out[:], warm_in[:], ACT.Sigmoid)
+
+        gn_sb = keep.tile([P, PACK], F32, name="gn_sb")
+        dsc_rows = d_scales[0].bitcast(I32)
+        xsc_rows = x_scales[0].bitcast(I32)
+        wsc_rows = w1_scales[0].bitcast(I32)
+        nc.sync.dma_start(kidx_sb[:], kidx)
+        nc.sync.dma_start(offs_sb[:], offs)
+        nc.sync.dma_start(n2_sb[:], n2)
+        nc.sync.dma_start(n1_sb[:], n1)
+        nc.sync.dma_start(gn_sb[:], gn.rearrange("(p t) o -> p (t o)", t=PACK))
+        for e in range(2):
+            nc.sync.dma_start(dsc_tab[e:P:LIST_ROWS, :].bitcast(I32), dsc_rows[e:16:2, :])
+        nc.sync.dma_start(d_tab[:], words_of(d_words))
+        for q in range(4):
+            nc.sync.dma_start(xsc_tab[32 * q : 32 * q + 4, :].bitcast(I32), xsc_rows[4 * q : 4 * q + 4, :])
+        nc.sync.dma_start(x_tab[:], words_of(x_words))
+
+        def deal(dst, src):
+            nc.vector.tensor_copy(
+                dst.rearrange("p (t m) -> p m t", t=PACK), src.rearrange("p (m t) -> p m t", t=PACK)
+            )
+
+        dsc_pick = keep.tile([P, S], U8, name="dsc_pick", tag="pick_then_wsc", align_bytes=64)
+        dsc = keep.tile([P, S], U8, name="dsc", align_bytes=64)
+        d_pick = keep.tile([P, S], I32, name="d_pick", align_bytes=64)
+        d_codes = keep.tile([P, S], I32, name="d_codes", align_bytes=64)
+        x_codes = keep.tile([P, S], I32, name="x_codes", align_bytes=64)
+        xsc = keep.tile([P, S], U8, name="xsc", align_bytes=64)
+        w_codes = keep.tile([P, S], I32, name="w_codes", align_bytes=64)
+        wsc = keep.tile([P, S], U8, name="wsc", align_bytes=64)
+
+        nc.vector.tensor_copy(dsc_pick[:], dsc_tab[:].indirect(kidx_sb[:]))
+        w_raw = keep.tile([P, S], I32, name="w_raw", tag="dsc_then_w", align_bytes=64)
+        nc.sync.dma_start(w_raw[:], words_of(w1_words))
+        deal(dsc[:], dsc_pick[:])
+        for e in range(2):
+            nc.scalar.dma_start(dsc[2 + e : P : 32, :].bitcast(I32), dsc[16 + e : P : 32, :].bitcast(I32))
+        wsc_raw = keep.tile([P, S], U8, name="wsc_raw", tag="pick_then_wsc", align_bytes=64)
+        nc.gpsimd.memset(wsc_raw[:].bitcast(I32), 0)
+        for q in range(4):
+            nc.sync.dma_start(wsc_raw[32 * q : 32 * q + 4, :].bitcast(I32), wsc_rows[4 * q : 4 * q + 4, :])
+        nc.vector.tensor_copy(d_pick[:].bitcast(U32), d_tab[:].bitcast(U32).indirect(kidx_sb[:]))
+        nc.vector.tensor_copy(xsc[:], xsc_tab[:].indirect(offs_sb[:]))
+        deal(d_codes[:], d_pick[:])
+        nc.vector.tensor_copy(x_codes[:].bitcast(U32), x_tab[:].bitcast(U32).indirect(offs_sb[:]))
+
+        scores = []
+        gs = keep.tile([P, PACK, S], F32, name="gs")
+        for t in range(PACK):
+            cols = slice(P * t, P * (t + 1))
+            acc = psum.tile([P, S], F32, name="score_acc%d" % t)
+            nc.tensor.matmul_mx(
+                out=acc[:], lhsT=d_codes[:, cols].bitcast(FP8X4), lhsT_scale=dsc[:, cols],
+                rhs=x_codes[:].bitcast(FP8X4), rhs_scale=xsc[:], start=True, stop=True,
+            )
+            s_t = keep.tile([P, S], F32, name="score%d" % t)
+            nc.scalar.activation(s_t[:], acc[:], ACT.Copy, scale=0.0625)
+            scores.append(s_t)
+        for t in range(PACK):
+            nc.scalar.activation(gs[:, t, :], scores[t][:], ACT.Copy, scale=gn_sb[:, t : t + 1])
+
+        out_rows = out_0.rearrange("(p t) j -> p t j", t=PACK)
+        out_words = words_of(out_1)
+        y_codes = keep.tile([P, S], I32, name="y_codes", align_bytes=64)
+        y_scales = keep.tile([P, S], U8, name="y_scales", align_bytes=64)
+
+        def compare(c, j0, n, between):
+            lst = slice(j0 // LIST_ROWS, (j0 + n) // LIST_ROWS)
+            low = keep.tile([P, PACK, n], F32, name="low%d" % c)
+            diff = keep.tile([P, PACK, n], F32, name="diff%d" % c)
+            gate = keep.tile([P, PACK, n], F32, name="gate%d" % c)
+            for t in range(PACK + 1):
+                if t < PACK:
+                    nc.vector.tensor_copy(low[:, t, :], scores[t][:].indirect(n2_sb[:, lst]))
+                if t > 0:
+                    u = t - 1
+                    nc.vector.tensor_tensor(diff[:, u, :], scores[u][:].indirect(n1_sb[:, lst]), low[:, u, :], ALU.subtract)
+                    nc.scalar.activation(gate[:, u, :], diff[:, u, :], ACT.Sigmoid)
+                between(t)
+            return gate
+
+        def weigh(c, j0, n, gate):
+            z = keep.tile([P, n, PACK], BF16, name="z%d" % c, align_bytes=64)
+            nc.vector.tensor_tensor(
+                z[:].rearrange("p (c i) t -> p c t i", i=4),
+                gate[:].rearrange("p t (c i) -> p c t i", i=4),
+                gs[:, :, j0 : j0 + n].rearrange("p t (c i) -> p c t i", i=4),
+                ALU.mult,
+            )
+            return z
+
+        def multiply(c, j0, n, z):
+            z_codes = keep.tile([P, n], I32, name="z_codes%d" % c, align_bytes=64)
+            z_scales = keep.tile([P, n], U8, name="z_scales%d" % c, align_bytes=64)
+            nc.vector.quantize_mx(
+                out=z_codes[:].bitcast(FP8X4), scales=z_scales[:], in_=z[:].rearrange("p j t -> p (j t)")
+            )
+            rounded = []
+            for h in range(n // P):
+                hc = slice(P * h, P * (h + 1))
+                acc = psum.tile([P, PACK, P], F32, name="out_acc%d" % (j0 // P + h))
+                for t in range(PACK):
+                    cols = slice(P * t, P * (t + 1))
+                    nc.tensor.matmul_mx(
+                        out=acc[:, t, :], lhsT=w_codes[:, cols].bitcast(FP8X4), lhsT_scale=wsc[:, cols],
+                        rhs=z_codes[:, hc].bitcast(FP8X4), rhs_scale=z_scales[:, hc], start=True, stop=True,
+                    )
+                y16 = keep.tile([P, P, PACK], BF16, name="y16_%d" % (j0 // P + h), align_bytes=64)
+                nc.scalar.copy(y16[:], acc[:].rearrange("p t j -> p j t"))
+                y = keep.tile([P, PACK, P], F32, name="y%d" % (j0 // P + h))
+                nc.scalar.copy(y[:], acc[:])
+                nc.sync.dma_start(out_rows[:, :, j0 + P * h : j0 + P * (h + 1)], y[:])
+                rounded.append((j0 + P * h, y16))
+            return rounded
+
+        def hand_on(rounded):
+            for j0, y16 in rounded:
+                cols = slice(j0, j0 + P)
+                nc.vector.quantize_mx(
+                    out=y_codes[:, cols].bitcast(FP8X4), scales=y_scales[:, cols],
+                    in_=y16[:].rearrange("p j t -> p (j t)"),
+                )
+                nc.sync.dma_start(out_words[:, cols], y_codes[:, cols])
+
+        starts = [sum(CHUNKS[:c]) for c in range(len(CHUNKS))]
+        gates, weighed, rounded = {}, {}, {}
+
+        def finish(c, t):
+            if c < 0:
+                if t == 3:
+                    deal(w_codes[:], w_raw[:])
+                    deal(wsc[:], wsc_raw[:])
+                return
+            if t == 1:
+                weighed[c] = weigh(c, starts[c], CHUNKS[c], gates[c])
+            if t == 2:
+                rounded[c] = multiply(c, starts[c], CHUNKS[c], weighed[c])
+            if t == 4:
+                hand_on(rounded[c])
+
+        for c in range(len(CHUNKS)):
+            gates[c] = compare(c, starts[c], CHUNKS[c], lambda t: finish(c - 1, t))
+        for t in range(PACK + 1):
+            finish(len(CHUNKS) - 1, t)
+
+        out_scale_rows = out_2[0].bitcast(I32)
+        for q in range(4):
+            queue = nc.sync if q % 2 == 0 else nc.scalar
+            queue.dma_start(out_scale_rows[4 * q : 4 * q + 4, :], y_scales[32 * q : 32 * q + 4, :].bitcast(I32))

@@ -64,9 +64,10 @@ def tile_picked_scorecmp_none_po_kernel(
             nc.sync.dma_start(xsc_tab[32 * q : 32 * q + 4, :].bitcast(I32), xsc_rows[4 * q : 4 * q + 4, :])
         nc.sync.dma_start(x_tab[:], words_of(x_words))
 
-        def deal(dst, src):
+        def deal(dst, src, run):
             nc.vector.tensor_copy(
-                dst.rearrange("p (t m) -> p m t", t=PACK), src.rearrange("p (m t) -> p m t", t=PACK)
+                dst.rearrange("p (t c i) -> p c t i", t=PACK, i=run),
+                src.rearrange("p (c i t) -> p c t i", t=PACK, i=run),
             )
 
         dsc_pick = keep.tile([P, S], U8, name="dsc_pick", tag="pick_then_wsc", align_bytes=64)
@@ -81,7 +82,7 @@ def tile_picked_scorecmp_none_po_kernel(
         nc.vector.tensor_copy(dsc_pick[:], dsc_tab[:].indirect(kidx_sb[:]))
         w_raw = keep.tile([P, S], I32, name="w_raw", tag="dsc_then_w", align_bytes=64)
         nc.sync.dma_start(w_raw[:], words_of(w1_words))
-        deal(dsc[:], dsc_pick[:])
+        deal(dsc[:], dsc_pick[:], 16)
         for e in range(2):
             nc.scalar.dma_start(dsc[2 + e : P : 32, :].bitcast(I32), dsc[16 + e : P : 32, :].bitcast(I32))
         wsc_raw = keep.tile([P, S], U8, name="wsc_raw", tag="pick_then_wsc", align_bytes=64)
@@ -90,50 +91,67 @@ def tile_picked_scorecmp_none_po_kernel(
             nc.sync.dma_start(wsc_raw[32 * q : 32 * q + 4, :].bitcast(I32), wsc_rows[4 * q : 4 * q + 4, :])
         nc.vector.tensor_copy(d_pick[:].bitcast(U32), d_tab[:].bitcast(U32).indirect(kidx_sb[:]))
         nc.vector.tensor_copy(xsc[:], xsc_tab[:].indirect(offs_sb[:]))
-        deal(d_codes[:], d_pick[:])
-        nc.vector.tensor_copy(x_codes[:].bitcast(U32), x_tab[:].bitcast(U32).indirect(offs_sb[:]))
-
-        scores = []
-        gs = keep.tile([P, PACK, S], F32, name="gs")
-        for t in range(PACK):
-            cols = slice(P * t, P * (t + 1))
-            acc = psum.tile([P, S], F32, name="score_acc%d" % t)
-            nc.tensor.matmul_mx(
-                out=acc[:], lhsT=d_codes[:, cols].bitcast(FP8X4), lhsT_scale=dsc[:, cols],
-                rhs=x_codes[:].bitcast(FP8X4), rhs_scale=xsc[:], start=True, stop=True,
+        deal(d_codes[:], d_pick[:], 4)
+        for h in range(2):
+            nc.vector.tensor_copy(
+                x_codes[:, 256 * h : 256 * (h + 1)].bitcast(U32),
+                x_tab[:].bitcast(U32).indirect(offs_sb[:, 16 * h : 16 * (h + 1)]),
             )
-            s_t = keep.tile([P, S], F32, name="score%d" % t)
-            nc.scalar.activation(s_t[:], acc[:], ACT.Copy, scale=0.0625)
-            scores.append(s_t)
-        for t in range(PACK):
-            nc.scalar.activation(gs[:, t, :], scores[t][:], ACT.Copy, scale=gn_sb[:, t : t + 1])
+        deal(w_codes[:], w_raw[:], 4)
+        deal(wsc[:], wsc_raw[:], 16)
+
+        scores = [keep.tile([P, S], F32, name="score%d" % t) for t in range(PACK)]
+        gs = [keep.tile([P, PACK, 256], F32, name="gs%d" % h) for h in range(2)]
+        for pair in range(2):
+            for h in range(2):
+                half = slice(256 * h, 256 * (h + 1))
+                for u in range(2):
+                    t = 2 * pair + u
+                    cols = slice(P * t, P * (t + 1))
+                    acc = psum.tile([P, 256], F32, name="bank%d" % (4 * pair + 2 * h + u))
+                    nc.tensor.matmul_mx(
+                        out=acc[:], lhsT=d_codes[:, cols].bitcast(FP8X4), lhsT_scale=dsc[:, cols],
+                        rhs=x_codes[:, half].bitcast(FP8X4), rhs_scale=xsc[:, half], start=True, stop=True,
+                    )
+                    nc.scalar.activation(scores[t][:, half], acc[:], ACT.Copy, scale=0.0625)
+
+        def weigh_scores(h):
+            half = slice(256 * h, 256 * (h + 1))
+            for t in range(PACK):
+                nc.scalar.activation(gs[h][:, t, :], scores[t][:, half], ACT.Copy, scale=gn_sb[:, t : t + 1])
+
+        weigh_scores(0)
 
         out_rows = out_0.rearrange("(p t) j -> p t j", t=PACK)
         out_words = words_of(out_1)
         y_codes = keep.tile([P, S], I32, name="y_codes", align_bytes=64)
         y_scales = keep.tile([P, S], U8, name="y_scales", align_bytes=64)
 
-        def compare(c, j0, n, between):
+        def fetch(j0, n):
             lst = slice(j0 // LIST_ROWS, (j0 + n) // LIST_ROWS)
-            low = keep.tile([P, PACK, n], F32, name="low%d" % c)
-            diff = keep.tile([P, PACK, n], F32, name="diff%d" % c)
-            gate = keep.tile([P, PACK, n], F32, name="gate%d" % c)
-            for t in range(PACK + 1):
-                if t < PACK:
-                    nc.vector.tensor_copy(low[:, t, :], scores[t][:].indirect(n2_sb[:, lst]))
-                if t > 0:
-                    u = t - 1
-                    nc.vector.tensor_tensor(diff[:, u, :], scores[u][:].indirect(n1_sb[:, lst]), low[:, u, :], ALU.subtract)
-                    nc.scalar.activation(gate[:, u, :], diff[:, u, :], ACT.Sigmoid)
-                between(t)
+            lows = []
+            for t in range(PACK):
+                low = keep.tile([P, n], F32, name="low%d" % t)
+                nc.vector.tensor_copy(low[:], scores[t][:].indirect(n2_sb[:, lst]))
+                lows.append(low)
+            return lows
+
+        def compare(j0, n, lows, between):
+            lst = slice(j0 // LIST_ROWS, (j0 + n) // LIST_ROWS)
+            gate = keep.tile([P, PACK, n], F32, name="gate")
+            for t in range(PACK):
+                nc.vector.tensor_tensor(gate[:, t, :], scores[t][:].indirect(n1_sb[:, lst]), lows[t][:], ALU.subtract)
+                nc.scalar.activation(gate[:, t, :], gate[:, t, :], ACT.Sigmoid)
+                if t == 0:
+                    between()
             return gate
 
         def weigh(c, j0, n, gate):
             z = keep.tile([P, n, PACK], BF16, name="z%d" % c, align_bytes=64)
             nc.vector.tensor_tensor(
-                z[:].rearrange("p (c i) t -> p c t i", i=4),
-                gate[:].rearrange("p t (c i) -> p c t i", i=4),
-                gs[:, :, j0 : j0 + n].rearrange("p t (c i) -> p c t i", i=4),
+                z[:].rearrange("p (c i) t -> p c t i", i=2),
+                gate[:].rearrange("p t (c i) -> p c t i", i=2),
+                gs[j0 // 256][:, :, j0 % 256 : j0 % 256 + n].rearrange("p t (c i) -> p c t i", i=2),
                 ALU.mult,
             )
             return z
@@ -144,27 +162,32 @@ def tile_picked_scorecmp_none_po_kernel(
             nc.vector.quantize_mx(
                 out=z_codes[:].bitcast(FP8X4), scales=z_scales[:], in_=z[:].rearrange("p j t -> p (j t)")
             )
-            rounded = []
+            sums = []
             for h in range(n // P):
                 hc = slice(P * h, P * (h + 1))
-                acc = psum.tile([P, PACK, P], F32, name="out_acc%d" % (j0 // P + h))
+                acc = psum.tile([P, PACK, P], F32, name="bank%d" % (j0 // P + h))
                 for t in range(PACK):
                     cols = slice(P * t, P * (t + 1))
                     nc.tensor.matmul_mx(
                         out=acc[:, t, :], lhsT=w_codes[:, cols].bitcast(FP8X4), lhsT_scale=wsc[:, cols],
                         rhs=z_codes[:, hc].bitcast(FP8X4), rhs_scale=z_scales[:, hc], start=True, stop=True,
                     )
-                y16 = keep.tile([P, P, PACK], BF16, name="y16_%d" % (j0 // P + h), align_bytes=64)
-                nc.scalar.copy(y16[:], acc[:].rearrange("p t j -> p j t"))
-                y = keep.tile([P, PACK, P], F32, name="y%d" % (j0 // P + h))
-                nc.scalar.copy(y[:], acc[:])
-                nc.sync.dma_start(out_rows[:, :, j0 + P * h : j0 + P * (h + 1)], y[:])
-                rounded.append((j0 + P * h, y16))
-            return rounded
+                sums.append((j0 + P * h, acc))
+            return sums
 
-        def hand_on(rounded):
-            for j0, y16 in rounded:
+        def hand_on(sums):
+            for j0, acc in sums:
                 cols = slice(j0, j0 + P)
+                y = keep.tile([P, PACK, P], F32, name="y%d" % (j0 // P))
+                y16 = keep.tile([P, P, PACK], BF16, name="y16_%d" % (j0 // P), align_bytes=64)
+                nc.scalar.copy(y[:], acc[:])
+                nc.sync.dma_start(out_rows[:, :, cols], y[:])
+                if j0 + P < S:
+                    nc.scalar.copy(y16[:], acc[:].rearrange("p t j -> p j t"))
+                else:
+                    nc.vector.tensor_copy(
+                        y16[:].rearrange("p (c i) t -> p c t i", i=2), y[:].rearrange("p t (c i) -> p c t i", i=2)
+                    )
                 nc.vector.quantize_mx(
                     out=y_codes[:, cols].bitcast(FP8X4), scales=y_scales[:, cols],
                     in_=y16[:].rearrange("p j t -> p (j t)"),
@@ -172,25 +195,25 @@ def tile_picked_scorecmp_none_po_kernel(
                 nc.sync.dma_start(out_words[:, cols], y_codes[:, cols])
 
         starts = [sum(CHUNKS[:c]) for c in range(len(CHUNKS))]
-        gates, weighed, rounded = {}, {}, {}
+        last = len(CHUNKS) - 1
+        gate, weighed, rounded = None, {}, {}
 
-        def finish(c, t):
-            if c < 0:
-                if t == 3:
-                    deal(w_codes[:], w_raw[:])
-                    deal(wsc[:], wsc_raw[:])
-                return
-            if t == 1:
-                weighed[c] = weigh(c, starts[c], CHUNKS[c], gates[c])
-            if t == 2:
+        def second_product(c):
+            if c >= 0:
                 rounded[c] = multiply(c, starts[c], CHUNKS[c], weighed[c])
-            if t == 4:
-                hand_on(rounded[c])
 
         for c in range(len(CHUNKS)):
-            gates[c] = compare(c, starts[c], CHUNKS[c], lambda t: finish(c - 1, t))
-        for t in range(PACK + 1):
-            finish(len(CHUNKS) - 1, t)
+            lows = fetch(starts[c], CHUNKS[c])
+            if c > 0:
+                weighed[c - 1] = weigh(c - 1, starts[c - 1], CHUNKS[c - 1], gate)
+            gate = compare(starts[c], CHUNKS[c], lows, lambda: second_product(c - 1))
+            if c > 0:
+                hand_on(rounded[c - 1])
+            if c == 0:
+                weigh_scores(1)
+        weighed[last] = weigh(last, starts[last], CHUNKS[last], gate)
+        second_product(last)
+        hand_on(rounded[last])
 
         out_scale_rows = out_2[0].bitcast(I32)
         for q in range(4):

@@ -36,15 +36,16 @@ def tile_picked_scorecmp_none_po_kernel(
         offs_sb = keep.tile([P, S // LIST_ROWS], U16, name="offs_sb")
         n1_sb = keep.tile([P, S // LIST_ROWS], U16, name="n1_sb")
         n2_sb = keep.tile([P, S // LIST_ROWS], U16, name="n2_sb")
-        d_tab = keep.tile([P, TABLE], I32, name="d_tab", align_bytes=64)
+        d_tab = keep.tile([P, TABLE], I32, name="d_tab", tag="d_then_wsc", align_bytes=64)
         x_tab = keep.tile([P, TABLE], I32, name="x_tab", align_bytes=64)
-        dsc_tab = keep.tile([P, TABLE], U8, name="dsc_tab", tag="dsc_then_w", align_bytes=64)
+        dsc_tab = keep.tile([P, TABLE], U8, name="dsc_tab", align_bytes=64)
         xsc_tab = keep.tile([P, TABLE], U8, name="xsc_tab", align_bytes=64)
         warm_in = keep.tile([P, 1], F32, name="warm_in")
         warm_out = keep.tile([P, 1], F32, name="warm_out")
 
         nc.gpsimd.memset(dsc_tab[:].bitcast(I32), 0)
-        nc.vector.memset(xsc_tab[:].bitcast(I32), 0)
+        nc.vector.memset(xsc_tab[:, :1536].bitcast(I32), 0)
+        nc.gpsimd.memset(xsc_tab[:, 1536:].bitcast(I32), 0)
         nc.vector.memset(warm_in[:], 0.0)
         nc.scalar.activation(warm_out[:], warm_in[:], ACT.Sigmoid)
 
@@ -54,15 +55,15 @@ def tile_picked_scorecmp_none_po_kernel(
         wsc_rows = w1_scales[0].bitcast(I32)
         nc.sync.dma_start(kidx_sb[:], kidx)
         nc.sync.dma_start(offs_sb[:], offs)
+        nc.sync.dma_start(gn_sb[:], gn.rearrange("(p t) o -> p (t o)", t=PACK))
+        for a in range(2):
+            nc.sync.dma_start(d_tab[:, 128 * a : 128 * (a + 1)], words_of(d_words)[:, 128 * a : 128 * (a + 1)])
+        nc.sync.dma_start(dsc_tab[0:P:8, :].bitcast(I32), dsc_rows)
+        nc.sync.dma_start(xsc_tab[0:P:8, :].bitcast(I32), xsc_rows)
+        nc.sync.dma_start(d_tab[:, 256:], words_of(d_words)[:, 256:])
+        nc.sync.dma_start(x_tab[:], words_of(x_words))
         nc.sync.dma_start(n2_sb[:], n2)
         nc.sync.dma_start(n1_sb[:], n1)
-        nc.sync.dma_start(gn_sb[:], gn.rearrange("(p t) o -> p (t o)", t=PACK))
-        for e in range(2):
-            nc.sync.dma_start(dsc_tab[e:P:LIST_ROWS, :].bitcast(I32), dsc_rows[e:16:2, :])
-        nc.sync.dma_start(d_tab[:], words_of(d_words))
-        for q in range(4):
-            nc.sync.dma_start(xsc_tab[32 * q : 32 * q + 4, :].bitcast(I32), xsc_rows[4 * q : 4 * q + 4, :])
-        nc.sync.dma_start(x_tab[:], words_of(x_words))
 
         def deal(dst, src, run):
             nc.vector.tensor_copy(
@@ -70,28 +71,30 @@ def tile_picked_scorecmp_none_po_kernel(
                 src.rearrange("p (c i t) -> p c t i", t=PACK, i=run),
             )
 
-        dsc_pick = keep.tile([P, S], U8, name="dsc_pick", tag="pick_then_wsc", align_bytes=64)
-        dsc = keep.tile([P, S], U8, name="dsc", align_bytes=64)
+        dsc_pick = keep.tile([P, S], U8, name="dsc_pick", align_bytes=64)
+        xsc_pick = keep.tile([P, S], U8, name="xsc_pick", tag="pick_then_w", align_bytes=64)
+        planes = keep.tile([P, 2 * S], U8, name="planes", align_bytes=64)
+        dsc, xsc = planes[:, :S], planes[:, S:]
         d_pick = keep.tile([P, S], I32, name="d_pick", align_bytes=64)
         d_codes = keep.tile([P, S], I32, name="d_codes", align_bytes=64)
         x_codes = keep.tile([P, S], I32, name="x_codes", align_bytes=64)
-        xsc = keep.tile([P, S], U8, name="xsc", align_bytes=64)
         w_codes = keep.tile([P, S], I32, name="w_codes", align_bytes=64)
         wsc = keep.tile([P, S], U8, name="wsc", align_bytes=64)
 
         nc.vector.tensor_copy(dsc_pick[:], dsc_tab[:].indirect(kidx_sb[:]))
-        w_raw = keep.tile([P, S], I32, name="w_raw", tag="dsc_then_w", align_bytes=64)
-        nc.sync.dma_start(w_raw[:], words_of(w1_words))
-        deal(dsc[:], dsc_pick[:], 16)
-        for e in range(2):
-            nc.scalar.dma_start(dsc[2 + e : P : 32, :].bitcast(I32), dsc[16 + e : P : 32, :].bitcast(I32))
-        wsc_raw = keep.tile([P, S], U8, name="wsc_raw", tag="pick_then_wsc", align_bytes=64)
+        nc.vector.tensor_copy(xsc_pick[:], xsc_tab[:].indirect(offs_sb[:]))
+        deal(dsc, dsc_pick[:], 16)
+        nc.vector.tensor_copy(xsc.bitcast(I32), xsc_pick[:].bitcast(I32))
+        for a in range(1, 4):
+            nc.scalar.dma_start(planes[a:P:32, :].bitcast(I32), planes[8 * a : P : 32, :].bitcast(I32))
+        w_raw = keep.tile([P, S], I32, name="w_raw", tag="pick_then_w", align_bytes=64)
+        nc.scalar.dma_start(w_raw[:], words_of(w1_words))
+        nc.vector.tensor_copy(d_pick[:].bitcast(U32), d_tab[:].bitcast(U32).indirect(kidx_sb[:]))
+        deal(d_codes[:], d_pick[:], 4)
+        wsc_raw = keep.tile([P, S], U8, name="wsc_raw", tag="d_then_wsc", align_bytes=64)
         nc.gpsimd.memset(wsc_raw[:].bitcast(I32), 0)
         for q in range(4):
             nc.sync.dma_start(wsc_raw[32 * q : 32 * q + 4, :].bitcast(I32), wsc_rows[4 * q : 4 * q + 4, :])
-        nc.vector.tensor_copy(d_pick[:].bitcast(U32), d_tab[:].bitcast(U32).indirect(kidx_sb[:]))
-        nc.vector.tensor_copy(xsc[:], xsc_tab[:].indirect(offs_sb[:]))
-        deal(d_codes[:], d_pick[:], 4)
         for h in range(2):
             nc.vector.tensor_copy(
                 x_codes[:, 256 * h : 256 * (h + 1)].bitcast(U32),
@@ -165,29 +168,29 @@ def tile_picked_scorecmp_none_po_kernel(
             sums = []
             for h in range(n // P):
                 hc = slice(P * h, P * (h + 1))
-                acc = psum.tile([P, PACK, P], F32, name="bank%d" % (j0 // P + h))
-                for t in range(PACK):
-                    cols = slice(P * t, P * (t + 1))
-                    nc.tensor.matmul_mx(
-                        out=acc[:, t, :], lhsT=w_codes[:, cols].bitcast(FP8X4), lhsT_scale=wsc[:, cols],
-                        rhs=z_codes[:, hc].bitcast(FP8X4), rhs_scale=z_scales[:, hc], start=True, stop=True,
-                    )
-                sums.append((j0 + P * h, acc))
+                accs = []
+                for pair in range(2):
+                    acc = psum.tile([P, 2, P], F32, name="bank%d" % (2 * (j0 // P + h) + pair))
+                    for u in range(2):
+                        cols = slice(P * (2 * pair + u), P * (2 * pair + u + 1))
+                        nc.tensor.matmul_mx(
+                            out=acc[:, u, :], lhsT=w_codes[:, cols].bitcast(FP8X4), lhsT_scale=wsc[:, cols],
+                            rhs=z_codes[:, hc].bitcast(FP8X4), rhs_scale=z_scales[:, hc], start=True, stop=True,
+                        )
+                    accs.append(acc)
+                sums.append((j0 + P * h, accs))
             return sums
 
         def hand_on(sums):
-            for j0, acc in sums:
+            for j0, accs in sums:
                 cols = slice(j0, j0 + P)
                 y = keep.tile([P, PACK, P], F32, name="y%d" % (j0 // P))
                 y16 = keep.tile([P, P, PACK], BF16, name="y16_%d" % (j0 // P), align_bytes=64)
-                nc.scalar.copy(y[:], acc[:])
+                for pair in range(2):
+                    nc.scalar.copy(y[:, 2 * pair : 2 * pair + 2, :], accs[pair][:])
                 nc.sync.dma_start(out_rows[:, :, cols], y[:])
-                if j0 + P < S:
-                    nc.scalar.copy(y16[:], acc[:].rearrange("p t j -> p j t"))
-                else:
-                    nc.vector.tensor_copy(
-                        y16[:].rearrange("p (c i) t -> p c t i", i=2), y[:].rearrange("p t (c i) -> p c t i", i=2)
-                    )
+                round_copy = nc.scalar.copy if j0 + P < S else nc.vector.tensor_copy
+                round_copy(y16[:].rearrange("p (c i) t -> p c t i", i=2), y[:].rearrange("p t (c i) -> p c t i", i=2))
                 nc.vector.quantize_mx(
                     out=y_codes[:, cols].bitcast(FP8X4), scales=y_scales[:, cols],
                     in_=y16[:].rearrange("p j t -> p (j t)"),
@@ -217,5 +220,5 @@ def tile_picked_scorecmp_none_po_kernel(
 
         out_scale_rows = out_2[0].bitcast(I32)
         for q in range(4):
-            queue = nc.sync if q % 2 == 0 else nc.scalar
+            queue = nc.sync if q == 3 else nc.scalar
             queue.dma_start(out_scale_rows[4 * q : 4 * q + 4, :], y_scales[32 * q : 32 * q + 4, :].bitcast(I32))

from contextlib import ExitStack

import concourse.mybir as mybir

F32 = mybir.dt.float32
BF16 = mybir.dt.bfloat16
I32 = mybir.dt.int32
U32 = mybir.dt.uint32
U16 = mybir.dt.uint16
U8 = mybir.dt.uint8
FP8X4 = mybir.dt.float8_e4m3fn_x4
ACT = mybir.ActivationFunctionType
ALU = mybir.AluOpType

P = 128
PACK = 4
TABLE = 2048
S = 512
LIST_ROWS = 16
CHUNKS = (256, 128, 128)
FLOPS = 2 * 2 * 512 * 512 * 512


def tile_picked_scorecmp_none_po_kernel(
    tc, x_words, x_scales, d_words, d_scales, gn, w1_words, w1_scales, offs, kidx, n1, n2, out_0, out_1, out_2
):
    nc = tc.nc
    with ExitStack() as ctx:
        keep = ctx.enter_context(tc.tile_pool(name="keep", bufs=1))
        psum = ctx.enter_context(tc.psum_pool(name="psum", bufs=1))

        def words_of(dram):
            return dram[0].rearrange("p c r -> p (c r)").bitcast(I32)

        kidx_sb = keep.tile([P, S // LIST_ROWS], U16, name="kidx_sb")
        offs_sb = keep.tile([P, S // LIST_ROWS], U16, name="offs_sb")
        n1_sb = keep.tile([P, S // LIST_ROWS], U16, name="n1_sb")
        n2_sb = keep.tile([P, S // LIST_ROWS], U16, name="n2_sb")
        d_tab = keep.tile([P, TABLE], I32, name="d_tab", tag="d_then_wsc", align_bytes=64)
        x_tab = keep.tile([P, TABLE], I32, name="x_tab", align_bytes=64)
        dsc_tab = keep.tile([P, TABLE], U8, name="dsc_tab", align_bytes=64)
        xsc_tab = keep.tile([P, TABLE], U8, name="xsc_tab", align_bytes=64)
        warm_in = keep.tile([P, 1], F32, name="warm_in")
        warm_out = keep.tile([P, 1], F32, name="warm_out")

        nc.gpsimd.memset(dsc_tab[:].bitcast(I32), 0)
        nc.vector.memset(xsc_tab[:, :1536].bitcast(I32), 0)
        nc.gpsimd.memset(xsc_tab[:, 1536:].bitcast(I32), 0)
        nc.vector.memset(warm_in[:], 0.0)
        nc.scalar.activation(warm_out[:], warm_in[:], ACT.Sigmoid)

        gn_sb = keep.tile([P, PACK], F32, name="gn_sb")
        dsc_rows = d_scales[0].bitcast(I32)
        xsc_rows = x_scales[0].bitcast(I32)
        wsc_rows = w1_scales[0].bitcast(I32)
        nc.sync.dma_start(kidx_sb[:], kidx)
        nc.sync.dma_start(offs_sb[:], offs)
        nc.sync.dma_start(gn_sb[:], gn.rearrange("(p t) o -> p (t o)", t=PACK))
        for a in range(2):
            nc.sync.dma_start(d_tab[:, 128 * a : 128 * (a + 1)], words_of(d_words)[:, 128 * a : 128 * (a + 1)])
        nc.sync.dma_start(dsc_tab[0:P:8, :].bitcast(I32), dsc_rows)
        nc.sync.dma_start(xsc_tab[0:P:8, :].bitcast(I32), xsc_rows)
        nc.sync.dma_start(d_tab[:, 256:], words_of(d_words)[:, 256:])
        nc.sync.dma_start(x_tab[:], words_of(x_words))
        nc.sync.dma_start(n2_sb[:], n2)
        nc.sync.dma_start(n1_sb[:], n1)

        def deal(dst, src, run):
            nc.vector.tensor_copy(
                dst.rearrange("p (t c i) -> p c t i", t=PACK, i=run),
                src.rearrange("p (c i t) -> p c t i", t=PACK, i=run),
            )

        dsc_pick = keep.tile([P, S], U8, name="dsc_pick", align_bytes=64)
        xsc_pick = keep.tile([P, S], U8, name="xsc_pick", tag="pick_then_w", align_bytes=64)
        planes = keep.tile([P, 2 * S], U8, name="planes", align_bytes=64)
        dsc, xsc = planes[:, :S], planes[:, S:]
        d_pick = keep.tile([P, S], I32, name="d_pick", align_bytes=64)
        d_codes = keep.tile([P, S], I32, name="d_codes", align_bytes=64)
        x_codes = keep.tile([P, S], I32, name="x_codes", align_bytes=64)
        w_codes = keep.tile([P, S], I32, name="w_codes", align_bytes=64)
        wsc = keep.tile([P, S], U8, name="wsc", align_bytes=64)

        nc.vector.tensor_copy(dsc_pick[:], dsc_tab[:].indirect(kidx_sb[:]))
        nc.vector.tensor_copy(xsc_pick[:], xsc_tab[:].indirect(offs_sb[:]))
        deal(dsc, dsc_pick[:], 16)
        nc.vector.tensor_copy(xsc.bitcast(I32), xsc_pick[:].bitcast(I32))
        for a in range(1, 4):
            nc.scalar.dma_start(planes[a:P:32, :].bitcast(I32), planes[8 * a : P : 32, :].bitcast(I32))
        w_raw = keep.tile([P, S], I32, name="w_raw", tag="pick_then_w", align_bytes=64)
        nc.scalar.dma_start(w_raw[:], words_of(w1_words))
        nc.vector.tensor_copy(d_pick[:].bitcast(U32), d_tab[:].bitcast(U32).indirect(kidx_sb[:]))
        deal(d_codes[:], d_pick[:], 4)
        wsc_raw = keep.tile([P, S], U8, name="wsc_raw", tag="d_then_wsc", align_bytes=64)
        nc.gpsimd.memset(wsc_raw[:].bitcast(I32), 0)
        for q in range(4):
            nc.sync.dma_start(wsc_raw[32 * q : 32 * q + 4, :].bitcast(I32), wsc_rows[4 * q : 4 * q + 4, :])
        for h in range(2):
            nc.vector.tensor_copy(
                x_codes[:, 256 * h : 256 * (h + 1)].bitcast(U32),
                x_tab[:].bitcast(U32).indirect(offs_sb[:, 16 * h : 16 * (h + 1)]),
            )
        deal(w_codes[:], w_raw[:], 4)
        deal(wsc[:], wsc_raw[:], 16)

        scores = [keep.tile([P, S], F32, name="score%d" % t) for t in range(PACK)]
        gs = [keep.tile([P, PACK, 256], F32, name="gs%d" % h) for h in range(2)]
        for pair in range(2):
            for h in range(2):
                half = slice(256 * h, 256 * (h + 1))
                for u in range(2):
                    t = 2 * pair + u
                    cols = slice(P * t, P * (t + 1))
                    acc = psum.tile([P, 256], F32, name="bank%d" % (4 * pair + 2 * h + u))
                    nc.tensor.matmul_mx(
                        out=acc[:], lhsT=d_codes[:, cols].bitcast(FP8X4), lhsT_scale=dsc[:, cols],
                        rhs=x_codes[:, half].bitcast(FP8X4), rhs_scale=xsc[:, half], start=True, stop=True,
                    )
                    nc.scalar.activation(scores[t][:, half], acc[:], ACT.Copy, scale=0.0625)

        def weigh_scores(h):
            half = slice(256 * h, 256 * (h + 1))
            for t in range(PACK):
                nc.scalar.activation(gs[h][:, t, :], scores[t][:, half], ACT.Copy, scale=gn_sb[:, t : t + 1])

        weigh_scores(0)

        out_rows = out_0.rearrange("(p t) j -> p t j", t=PACK)
        out_words = words_of(out_1)
        y_codes = keep.tile([P, S], I32, name="y_codes", align_bytes=64)
        y_scales = keep.tile([P, S], U8, name="y_scales", align_bytes=64)

        def fetch(j0, n):
            lst = slice(j0 // LIST_ROWS, (j0 + n) // LIST_ROWS)
            lows = []
            for t in range(PACK):
                low = keep.tile([P, n], F32, name="low%d" % t)
                nc.vector.tensor_copy(low[:], scores[t][:].indirect(n2_sb[:, lst]))
                lows.append(low)
            return lows

        def compare(j0, n, lows, between):
            lst = slice(j0 // LIST_ROWS, (j0 + n) // LIST_ROWS)
            gate = keep.tile([P, PACK, n], F32, name="gate")
            for t in range(PACK):
                nc.vector.tensor_tensor(gate[:, t, :], scores[t][:].indirect(n1_sb[:, lst]), lows[t][:], ALU.subtract)
                nc.scalar.activation(gate[:, t, :], gate[:, t, :], ACT.Sigmoid)
                if t == 0:
                    between()
            return gate

        def weigh(c, j0, n, gate):
            z = keep.tile([P, n, PACK], BF16, name="z%d" % c, align_bytes=64)
            nc.vector.tensor_tensor(
                z[:].rearrange("p (c i) t -> p c t i", i=2),
                gate[:].rearrange("p t (c i) -> p c t i", i=2),
                gs[j0 // 256][:, :, j0 % 256 : j0 % 256 + n].rearrange("p t (c i) -> p c t i", i=2),
                ALU.mult,
            )
            return z

        def multiply(c, j0, n, z):
            z_codes = keep.tile([P, n], I32, name="z_codes%d" % c, align_bytes=64)
            z_scales = keep.tile([P, n], U8, name="z_scales%d" % c, align_bytes=64)
            nc.vector.quantize_mx(
                out=z_codes[:].bitcast(FP8X4), scales=z_scales[:], in_=z[:].rearrange("p j t -> p (j t)")
            )
            sums = []
            for h in range(n // P):
                hc = slice(P * h, P * (h + 1))
                accs = []
                for pair in range(2):
                    acc = psum.tile([P, 2, P], F32, name="bank%d" % (2 * (j0 // P + h) + pair))
                    for u in range(2):
                        cols = slice(P * (2 * pair + u), P * (2 * pair + u + 1))
                        nc.tensor.matmul_mx(
                            out=acc[:, u, :], lhsT=w_codes[:, cols].bitcast(FP8X4), lhsT_scale=wsc[:, cols],
                            rhs=z_codes[:, hc].bitcast(FP8X4), rhs_scale=z_scales[:, hc], start=True, stop=True,
                        )
                    accs.append(acc)
                sums.append((j0 + P * h, accs))
            return sums

        def hand_on(sums):
            for j0, accs in sums:
                cols = slice(j0, j0 + P)
                y = keep.tile([P, PACK, P], F32, name="y%d" % (j0 // P))
                y16 = keep.tile([P, P, PACK], BF16, name="y16_%d" % (j0 // P), align_bytes=64)
                for pair in range(2):
                    nc.scalar.copy(y[:, 2 * pair : 2 * pair + 2, :], accs[pair][:])
                nc.sync.dma_start(out_rows[:, :, cols], y[:])
                round_copy = nc.scalar.copy if j0 + P < S else nc.vector.tensor_copy
                round_copy(y16[:].rearrange("p (c i) t -> p c t i", i=2), y[:].rearrange("p t (c i) -> p c t i", i=2))
                nc.vector.quantize_mx(
                    out=y_codes[:, cols].bitcast(FP8X4), scales=y_scales[:, cols],
                    in_=y16[:].rearrange("p j t -> p (j t)"),
                )
                nc.sync.dma_start(out_words[:, cols], y_codes[:, cols])

        starts = [sum(CHUNKS[:c]) for c in range(len(CHUNKS))]
        last = len(CHUNKS) - 1
        gate, weighed, rounded = None, {}, {}

        def second_product(c):
            if c >= 0:
                rounded[c] = multiply(c, starts[c], CHUNKS[c], weighed[c])

        for c in range(len(CHUNKS)):
            lows = fetch(starts[c], CHUNKS[c])
            if c > 0:
                weighed[c - 1] = weigh(c - 1, starts[c - 1], CHUNKS[c - 1], gate)
            gate = compare(starts[c], CHUNKS[c], lows, lambda: second_product(c - 1))
            if c > 0:
                hand_on(rounded[c - 1])
            if c == 0:
                weigh_scores(1)
        weighed[last] = weigh(last, starts[last], CHUNKS[last], gate)
        second_product(last)
        hand_on(rounded[last])

        out_scale_rows = out_2[0].bitcast(I32)
        for q in range(4):
            queue = nc.sync if q == 3 else nc.scalar
            queue.dma_start(out_scale_rows[4 * q : 4 * q + 4, :], y_scales[32 * q : 32 * q + 4, :].bitcast(I32))
